import numpy as np
import ml_dtypes


def mxq(x, axis, fmt="e4m3"):
    dtype, down = {"e4m3": (ml_dtypes.float8_e4m3fn, 7), "e5m2": (ml_dtypes.float8_e5m2, 14)}[fmt]
    v = np.moveaxis(np.asarray(x, np.float32).astype(ml_dtypes.bfloat16).astype(np.float64), axis, -1)
    blocks = v.reshape(v.shape[:-1] + (-1, 32))
    amax = np.abs(blocks).max(-1, keepdims=True)
    byte = np.maximum(np.where(amax > 0, np.frexp(amax)[1] - 1 + 127, 0) - down, 1)
    scale = np.exp2(byte - 127.0)
    codes = (blocks / scale).astype(np.float32).astype(dtype).astype(np.float64)
    return np.moveaxis((codes * scale).reshape(v.shape), -1, axis)


WIDE = False


def mx_kscale(k):
    if not WIDE:
        return np.ones(k)
    levels = np.array([10, -10, 5, -5, 0])
    if k % 512:
        return np.exp2(np.random.permutation(np.resize(levels, k // 32))).repeat(32)
    a = np.empty((k // 512, 16))
    for p in range(k // 512):
        a[p, :8] = np.random.permutation(np.resize(levels, 8))
        for g in range(8):
            far = levels[np.abs(levels - a[p, g]) >= 10]
            a[p, g + 8] = far[np.random.randint(len(far))]
    return np.exp2(a.ravel()).repeat(32)


def f64(x):
    return np.asarray(x).astype(np.float64)


def striped(idx):
    return np.tile(np.asarray(idx).reshape(-1, 16).T, (8, 1)).astype(np.uint16)


def unstriped(offs):
    return offs[:16].T.reshape(-1).astype(np.int64)


E2M1 = np.array([0.0, 0.5, 1.0, 1.5, 2.0, 3.0, 4.0, 6.0, -0.0, -0.5, -1.0, -1.5, -2.0, -3.0, -4.0, -6.0])


def pack_weight(w, fmt):
    k, n = w.shape
    w = f64(np.asarray(w, np.float32).astype(ml_dtypes.bfloat16)).reshape(k // 32, 32, n)
    amax = np.abs(w).max(1)
    if fmt == "e4m3":
        byte = np.frexp(amax)[1] - 1 + 127 - 7
    else:
        mant, ex = np.frexp(amax / 6.0)
        byte = np.where(mant > 0.5, ex, ex - 1) + 127
    byte = np.clip(np.where(amax > 0, byte, 1), 1, 254)
    scaled = (w * np.exp2(127.0 - byte)[:, None, :]).reshape(k, n).astype(np.float32)
    by_word = np.ascontiguousarray(scaled.reshape(k // 512, 128, 4, n).transpose(0, 1, 3, 2))
    if fmt == "e4m3":
        words = by_word.astype(ml_dtypes.float8_e4m3fn).view(np.uint8)
    else:
        c = by_word.astype(ml_dtypes.float4_e2m1fn).view(np.uint8) & 0xF
        words = (c[..., 0::2] | (c[..., 1::2] << 4)).reshape(k // 512, 128, 2 * n)
    return np.ascontiguousarray(words), np.ascontiguousarray(byte.astype(np.uint8).reshape(k // 512, 16, n))


def unpack_weight(words, scales, fmt):
    g, _, n = scales.shape
    words = np.ascontiguousarray(words).reshape(g, 128, n, -1)
    if fmt == "e4m3":
        vals = words.view(ml_dtypes.float8_e4m3fn).astype(np.float64)
    else:
        nib = np.empty((g, 128, n, 4), np.uint8)
        nib[..., 0::2] = words & 0xF
        nib[..., 1::2] = words >> 4
        vals = E2M1[nib]
    vals = vals * np.repeat(np.exp2(scales.astype(np.float64) - 127.0), 8, axis=1)[..., None]
    return vals.transpose(0, 1, 3, 2).reshape(g * 512, n)


def bf(x):
    return np.asarray(x, np.float32).astype(ml_dtypes.bfloat16)


def planes(Y):
    r, m = Y.shape
    b = f64(bf(Y)).reshape(r // 32, 32, m)
    amax = np.abs(b).max(1)
    byte = np.clip(np.where(amax > 0, np.frexp(amax)[1] - 1 + 127 - 7, 1), 1, 254)
    codes = (b * np.exp2(127.0 - byte)[:, None, :]).reshape(r, m).astype(np.float32).astype(ml_dtypes.float8_e4m3fn).view(np.uint8)
    words = codes.reshape(r // 512, 128, 4, m).transpose(0, 1, 3, 2)
    return np.ascontiguousarray(words), np.ascontiguousarray(byte.astype(np.uint8).reshape(r // 512, 16, m))


D, T, I, G, U, Q, E = 512, 4096, 2048, 512, 2048, 256, 512


def setup_inputs():
    n = np.random.standard_normal
    idx = np.random.permutation(T)[:I]
    idx2 = np.random.permutation(U)[:G]
    fd = mx_kscale(D)
    fg = mx_kscale(G)
    tg = np.ones(U)
    tg[idx2] = fg
    keysp = pack_weight(n((D, T)) / fd[:, None], "e2m1")
    return {
        "query": (n((D, Q)) * 0.25 / np.sqrt(D) * fd[:, None]).astype(np.float32),
        "keys_words": keysp[0],
        "keys_scales": keysp[1],
        "size": (np.random.uniform(0.5, 2.0, (1, G)) * fg).astype(np.float32),
        "vals": (n((E, U)) / tg).astype(np.float32),
        "offs": striped(idx),
        "offs2": striped(idx2),
    }


def reference(query, keys_words, keys_scales, size, vals, offs, offs2):
    idx = unstriped(offs)
    idx2 = unstriped(offs2)
    keysu = unpack_weight(keys_words, keys_scales, "e2m1")
    queryq = mxq(f64(query), 0, "e4m3")
    keysidxg = keysu[:, idx]
    a = queryq.T @ keysidxg
    s = a.reshape(Q, G, I // G).max(axis=2)
    p = np.exp(s - np.max(s, axis=1, keepdims=True))
    w = p * f64(size) / np.sum(p, axis=1, keepdims=True)
    wt = w.T
    vt = f64(vals)[:, idx2].T
    vtq = mxq(vt, 0, "e4m3")
    wtq = mxq(wt, 0, "e4m3")
    o = vtq.T @ wtq
    words, scales = planes(o)
    return o, words, scales

@@ -1,0 +1,230 @@
+from contextlib import ExitStack
+
+import concourse.mybir as mybir
+from concourse.masks import make_identity
+
+D, T, I, G, U, Q, E = 512, 4096, 2048, 512, 2048, 256, 512
+FLOPS = 2 * Q * I * D + 2 * E * Q * G
+
+F32 = mybir.dt.float32
+BF16 = mybir.dt.bfloat16
+I32 = mybir.dt.int32
+U32 = mybir.dt.uint32
+U16 = mybir.dt.uint16
+U8 = mybir.dt.uint8
+FP8X4 = mybir.dt.float8_e4m3fn_x4
+FP4X4 = mybir.dt.float4_e2m1fn_x4
+ALU = mybir.AluOpType
+ACT = mybir.ActivationFunctionType
+AX = mybir.AxisListType
+
+P = 128
+PACK = 4
+BANK = 512
+HALF = 1024
+ON_SCALAR = 2
+
+
+def tile_attend_wordmax_pl_kernel(tc, query, keys_words, keys_scales, size, vals, offs, offs2, out_0, out_1, out_2):
+    nc = tc.nc
+    with ExitStack() as ctx:
+        keep = ctx.enter_context(tc.tile_pool(name="keep", bufs=1))
+        ring = ctx.enter_context(tc.tile_pool(name="ring", bufs=2))
+        acc_pool = ctx.enter_context(tc.psum_pool(name="acc", bufs=6))
+        turn_pool = ctx.enter_context(tc.psum_pool(name="turn", bufs=2))
+
+        slots = keep.tile([P, I // 16], U16, name="slots")
+        entries = keep.tile([P, G // 16], U16, name="entries")
+        kw = keep.tile([P, T], U16, name="kw", align_bytes=64)
+        ks = keep.tile([P, T], U8, name="ks", align_bytes=64)
+        ks_words = ks[:].bitcast(I32)
+        nc.gpsimd.memset(ks_words[:, : T // 8], 0)
+        nc.vector.memset(ks_words[:, T // 8 :], 0)
+        warm = keep.tile([P, 1], F32, name="warm")
+        warm2 = keep.tile([P, 1], F32, name="warm2")
+        nc.vector.memset(warm[:], 0.0)
+        nc.scalar.activation(warm2[:], warm[:], ACT.Exp)
+
+        size_col = keep.tile([P, PACK], F32, name="size_col")
+        nc.sync.dma_start(slots[:], offs)
+        nc.sync.dma_start(entries[:], offs2)
+        nc.sync.dma_start(out=size_col[:], in_=size.rearrange("o (p t) -> (o p) t", t=PACK))
+        for quad in range(4):
+            nc.sync.dma_start(out=ks[32 * quad : 32 * quad + 4, :].bitcast(I32), in_=keys_scales[0, 4 * quad : 4 * quad + 4, :].bitcast(I32))
+        vals_rows = vals.rearrange("(p j) u -> j p u", j=PACK)
+        v_raw = {}
+
+        def load_values(j):
+            if j < ON_SCALAR:
+                for part in range(2):
+                    v_part = keep.tile([P, U // 2], F32, name=f"v_part{j}_{part}", align_bytes=64)
+                    nc.sync.dma_start(out=v_part[:], in_=vals_rows[j][:, part * U // 2 : (part + 1) * U // 2])
+                    v_raw[j, part] = v_part
+            else:
+                v_tile = keep.tile([P, U], F32, name=f"v_raw{j}", align_bytes=64)
+                nc.sync.dma_start(out=v_tile[:], in_=vals_rows[j])
+                v_raw[j] = v_tile
+
+        load_values(0)
+        nc.sync.dma_start(out=kw[:].bitcast(I32), in_=keys_words[0].bitcast(I32))
+        q_raw = keep.tile([P, PACK, Q], F32, name="q_raw")
+        nc.sync.dma_start(out=q_raw[:], in_=query.rearrange("(p j) q -> p j q", j=PACK))
+        load_values(1)
+        load_values(2)
+        load_values(3)
+
+        ident = keep.tile([P, P], F32, name="ident")
+        make_identity(nc, ident[:])
+
+        size_ps = turn_pool.tile([P, PACK, P], F32, name="turn")
+        for t in range(PACK):
+            nc.tensor.transpose(size_ps[:, t, :], size_col[:, t : t + 1].to_broadcast([P, P]), ident[:])
+        size_row = keep.tile([P, P, PACK], F32, name="size_row")
+        nc.scalar.copy(size_row[:], size_ps[:].rearrange("p t m -> p m t"))
+
+        q_bf = keep.tile([P, Q, PACK], BF16, name="q_bf", align_bytes=64)
+        nc.scalar.copy(q_bf[:], q_raw[:].rearrange("p j q -> p q j"))
+        q_codes = keep.tile([P, Q], U32, name="q_codes", align_bytes=64)
+        q_scales = keep.tile([P, Q], U8, name="q_scales", align_bytes=64)
+
+        v_in = keep.tile([P, PACK, P, PACK], BF16, name="v_in", align_bytes=64)
+        v_codes = keep.tile([P, E], U32, name="v_codes", align_bytes=64)
+        v_scales = keep.tile([P, E], U8, name="v_scales", align_bytes=64)
+
+        def turn(rows_bf, dest):
+            words = rows_bf[:].bitcast(F32)
+            bank = turn_pool.tile([P, 2, P], F32, name="turn")
+            for u in range(2):
+                nc.tensor.transpose(bank[:, u, :], words[:, u : G // 2 : 2], ident[:])
+            nc.scalar.copy(dest.bitcast(F32), bank[:].rearrange("p u r -> p r u"))
+
+        v_bf = {}
+
+        def cast_values(j):
+            v_bf[j] = keep.tile([P, U], BF16, name=f"v_bf{j}", align_bytes=64)
+            for part in range(2):
+                nc.scalar.activation(v_bf[j][:, part * U // 2 : (part + 1) * U // 2], v_raw[j, part][:], ACT.Copy)
+
+        def gather_values(j):
+            picked = keep.tile([P, G], BF16, name="pairs1" if j == 3 else f"v_picked{j}", align_bytes=64)
+            if j < ON_SCALAR:
+                nc.scalar.activation(picked[:], v_bf[j][:].indirect(entries[:]), ACT.Copy)
+            else:
+                nc.vector.tensor_copy(picked[:], v_raw[j][:].indirect(entries[:]))
+            turn(picked, v_in[:, j])
+
+        def quantize_values(j0, j1):
+            nc.vector.quantize_mx(
+                out=v_codes[:, j0 * P : j1 * P].bitcast(FP8X4),
+                scales=v_scales[:, j0 * P : j1 * P],
+                in_=v_in[:, j0:j1].rearrange("p j e t -> p (j e t)"),
+            )
+
+        gw, gs = [], []
+        for half in range(I // HALF):
+            cols = slice(half * HALF // 16, (half + 1) * HALF // 16)
+            gw_half = keep.tile([P, HALF], U16, name="q_bf" if half == 1 else "gw0", align_bytes=64)
+            gs_half = keep.tile([P, HALF], U8, name=f"gs{half}", align_bytes=64)
+            nc.vector.tensor_copy(gs_half[:], ks[:].indirect(slots[:, cols]))
+            nc.vector.tensor_copy(gw_half[:], kw[:].indirect(slots[:, cols]))
+            gw.append(gw_half)
+            gs.append(gs_half)
+            if half == 0:
+                nc.vector.quantize_mx(out=q_codes[:].bitcast(FP8X4), scales=q_scales[:], in_=q_bf[:].rearrange("p q j -> p (q j)"))
+
+        cast_values(0)
+        gather_values(0)
+        cast_values(1)
+        gather_values(2)
+
+        pairs = [keep.tile([P, 2, G], F32, name=f"pairs{h}", align_bytes=64) for h in range(2)]
+
+        def score(c, h):
+            half, lo_col = divmod(c * BANK, HALF)
+            bank = acc_pool.tile([P, BANK], F32, name="acc")
+            nc.tensor.matmul_mx(
+                out=bank[:],
+                lhsT=q_codes[:, h * P : (h + 1) * P].bitcast(FP8X4),
+                lhsT_scale=q_scales[:, h * P : (h + 1) * P],
+                rhs=gw[half][:, lo_col : lo_col + BANK].bitcast(FP4X4),
+                rhs_scale=gs[half][:, lo_col : lo_col + BANK],
+                start=True,
+                stop=True,
+            )
+            by_place = bank[:].rearrange("p (g r) -> p r g", r=PACK)
+            low = ring.tile([P, 2, P], F32, name="low", bufs=4)
+            nc.scalar.copy(low[:], by_place[:, 0:2, :])
+            nc.vector.tensor_tensor(pairs[h][:, :, c * P : (c + 1) * P], by_place[:, 2:4, :], low[:], ALU.max)
+
+        best, neg_max, prob, total = {}, {}, {}, {}
+
+        def softmax(h):
+            best[h] = keep.tile([P, G], F32, name=f"best{h}")[:]
+            neg_max[h] = keep.tile([P, 1], F32, name=f"neg_max{h}")
+            prob[h] = keep.tile([P, G], F32, name=f"prob{h}")
+            total[h] = keep.tile([P, 1], F32, name=f"total{h}")
+            nc.vector.tensor_tensor(best[h], pairs[h][:, 0, :], pairs[h][:, 1, :], ALU.max)
+            nc.vector.tensor_reduce(neg_max[h][:], best[h], AX.X, ALU.max, negate=True)
+            nc.scalar.activation(prob[h][:], best[h], ACT.Exp, bias=neg_max[h][:], accum_out=total[h][:])
+
+        w_in = keep.tile([P, 2, P, PACK], BF16, name="w_in", align_bytes=64)
+        w_codes = keep.tile([P, Q], U32, name="w_codes", align_bytes=64)
+        w_scales = keep.tile([P, Q], U8, name="w_scales", align_bytes=64)
+
+        def weigh(h):
+            inv = keep.tile([P, 1], F32, name=f"inv{h}")
+            nc.vector.reciprocal(inv[:], total[h][:])
+            w_bf = keep.tile([P, G], BF16, name=f"w_bf{h}", align_bytes=64)
+            nc.vector.scalar_tensor_tensor(w_bf[:], prob[h][:], inv[:], size_row[:].rearrange("p m t -> p (m t)"), ALU.mult, ALU.mult)
+            turn(w_bf, w_in[:, h])
+
+        def quantize_weights(h):
+            cols = slice(h * P, (h + 1) * P)
+            nc.vector.quantize_mx(out=w_codes[:, cols].bitcast(FP8X4), scales=w_scales[:, cols], in_=w_in[:, h].rearrange("p q t -> p (q t)"))
+
+        for c, h in ((0, 0), (1, 0), (0, 1), (1, 1), (2, 0), (3, 0)):
+            score(c, h)
+        softmax(0)
+        score(2, 1)
+        score(3, 1)
+        gather_values(1)
+        weigh(0)
+        softmax(1)
+        gather_values(3)
+        quantize_values(0, 2)
+        quantize_values(2, 3)
+        quantize_weights(0)
+        weigh(1)
+        quantize_values(3, 4)
+        quantize_weights(1)
+
+        o_codes = keep.tile([P, Q], U32, name="o_codes", align_bytes=64)
+        o_scales = keep.tile([P, Q], U8, name="o_scales", align_bytes=64)
+        out_rows = out_0.rearrange("(p j) q -> p j q", j=PACK)
+        out_words = out_1[0].rearrange("p q t -> p (q t)").bitcast(I32)
+        for h in range(2):
+            cols = slice(h * P, (h + 1) * P)
+            bank = acc_pool.tile([P, PACK, P], F32, name="acc")
+            for j in range(PACK):
+                nc.tensor.matmul_mx(
+                    out=bank[:, j, :],
+                    lhsT=v_codes[:, j * P : (j + 1) * P].bitcast(FP8X4),
+                    lhsT_scale=v_scales[:, j * P : (j + 1) * P],
+                    rhs=w_codes[:, cols].bitcast(FP8X4),
+                    rhs_scale=w_scales[:, cols],
+                    start=True,
+                    stop=True,
+                )
+            o_f32 = keep.tile([P, PACK, P], F32, name=f"o_f32_{h}")
+            o_bf = keep.tile([P, P, PACK], BF16, name=f"o_bf{h}", align_bytes=64)
+            if h == 1:
+                nc.vector.tensor_copy(o_bf[:], bank[:].rearrange("p j q -> p q j"))
+            nc.scalar.copy(o_f32[:], bank[:])
+            nc.sync.dma_start(out=out_rows[:, :, cols], in_=o_f32[:])
+            if h == 0:
+                nc.vector.tensor_copy(o_bf[:], o_f32[:].rearrange("p j q -> p q j"))
+            nc.vector.quantize_mx(out=o_codes[:, cols].bitcast(FP8X4), scales=o_scales[:, cols], in_=o_bf[:].rearrange("p q j -> p (q j)"))
+            nc.sync.dma_start(out=out_words[:, cols], in_=o_codes[:, cols].bitcast(I32))
+        for quad in range(4):
+            queue = nc.scalar if quad % 2 else nc.sync
+            queue.dma_start(out=out_2[0, 4 * quad : 4 * quad + 4, :].bitcast(I32), in_=o_scales[32 * quad : 32 * quad + 4, :].bitcast(I32))

@@ -22,24 +22,21 @@ P = 128
 PACK = 4
 BANK = 512
 HALF = 1024
-ON_SCALAR = 2
+ON_SCALAR = 3
 
 
 def tile_attend_wordmax_pl_kernel(tc, query, keys_words, keys_scales, size, vals, offs, offs2, out_0, out_1, out_2):
     nc = tc.nc
     with ExitStack() as ctx:
         keep = ctx.enter_context(tc.tile_pool(name="keep", bufs=1))
-        ring = ctx.enter_context(tc.tile_pool(name="ring", bufs=2))
-        acc_pool = ctx.enter_context(tc.psum_pool(name="acc", bufs=6))
-        turn_pool = ctx.enter_context(tc.psum_pool(name="turn", bufs=2))
+        psum = ctx.enter_context(tc.psum_pool(name="psum", bufs=1))
 
         slots = keep.tile([P, I // 16], U16, name="slots")
         entries = keep.tile([P, G // 16], U16, name="entries")
         kw = keep.tile([P, T], U16, name="kw", align_bytes=64)
         ks = keep.tile([P, T], U8, name="ks", align_bytes=64)
         ks_words = ks[:].bitcast(I32)
-        nc.gpsimd.memset(ks_words[:, : T // 8], 0)
-        nc.vector.memset(ks_words[:, T // 8 :], 0)
+        nc.vector.memset(ks_words[0:112, :], 0)
         warm = keep.tile([P, 1], F32, name="warm")
         warm2 = keep.tile([P, 1], F32, name="warm2")
         nc.vector.memset(warm[:], 0.0)
@@ -47,36 +44,34 @@ def tile_attend_wordmax_pl_kernel(tc, query, keys_words, keys_scales, size, vals
 
         size_col = keep.tile([P, PACK], F32, name="size_col")
         nc.sync.dma_start(slots[:], offs)
-        nc.sync.dma_start(entries[:], offs2)
-        nc.sync.dma_start(out=size_col[:], in_=size.rearrange("o (p t) -> (o p) t", t=PACK))
-        for quad in range(4):
-            nc.sync.dma_start(out=ks[32 * quad : 32 * quad + 4, :].bitcast(I32), in_=keys_scales[0, 4 * quad : 4 * quad + 4, :].bitcast(I32))
+        nc.sync.dma_start(out=ks_words[112:128, :], in_=keys_scales[0].bitcast(I32))
+        nc.scalar.dma_start(out=size_col[:], in_=size.rearrange("o (p t) -> (o p) t", t=PACK))
         vals_rows = vals.rearrange("(p j) u -> j p u", j=PACK)
         v_raw = {}
 
-        def load_values(j):
+        def load_values(j, parts=(0, 1)):
             if j < ON_SCALAR:
-                for part in range(2):
-                    v_part = keep.tile([P, U // 2], F32, name=f"v_part{j}_{part}", align_bytes=64)
+                for part in parts:
+                    v_part = keep.tile([P, U // 2], F32, name=(("v_part0", "v_part1"), ("v_part2", "ks"), ("v_bf0", "q_raw"))[j][part], align_bytes=64)
                     nc.sync.dma_start(out=v_part[:], in_=vals_rows[j][:, part * U // 2 : (part + 1) * U // 2])
                     v_raw[j, part] = v_part
             else:
-                v_tile = keep.tile([P, U], F32, name=f"v_raw{j}", align_bytes=64)
+                v_tile = keep.tile([P, U], F32, name="gs_rows", align_bytes=64)
                 nc.sync.dma_start(out=v_tile[:], in_=vals_rows[j])
                 v_raw[j] = v_tile
 
         load_values(0)
+        nc.sync.dma_start(entries[:], offs2)
         nc.sync.dma_start(out=kw[:].bitcast(I32), in_=keys_words[0].bitcast(I32))
-        q_raw = keep.tile([P, PACK, Q], F32, name="q_raw")
+        q_raw = keep.tile([P, PACK, Q], F32, name="q_raw", align_bytes=64)
         nc.sync.dma_start(out=q_raw[:], in_=query.rearrange("(p j) q -> p j q", j=PACK))
-        load_values(1)
-        load_values(2)
-        load_values(3)
+
+        load_values(1, (0,))
 
         ident = keep.tile([P, P], F32, name="ident")
         make_identity(nc, ident[:])
 
-        size_ps = turn_pool.tile([P, PACK, P], F32, name="turn")
+        size_ps = psum.tile([P, PACK, P], F32, name="bank6")
         for t in range(PACK):
             nc.tensor.transpose(size_ps[:, t, :], size_col[:, t : t + 1].to_broadcast([P, P]), ident[:])
         size_row = keep.tile([P, P, PACK], F32, name="size_row")
@@ -88,86 +83,96 @@ def tile_attend_wordmax_pl_kernel(tc, query, keys_words, keys_scales, size, vals
         q_scales = keep.tile([P, Q], U8, name="q_scales", align_bytes=64)
 
         v_in = keep.tile([P, PACK, P, PACK], BF16, name="v_in", align_bytes=64)
-        v_codes = keep.tile([P, E], U32, name="v_codes", align_bytes=64)
+        v_codes = {}
         v_scales = keep.tile([P, E], U8, name="v_scales", align_bytes=64)
 
-        def turn(rows_bf, dest):
+        def turn(rows_bf, dest, bank_name):
             words = rows_bf[:].bitcast(F32)
-            bank = turn_pool.tile([P, 2, P], F32, name="turn")
+            bank = psum.tile([P, 2, P], F32, name=bank_name)
             for u in range(2):
                 nc.tensor.transpose(bank[:, u, :], words[:, u : G // 2 : 2], ident[:])
             nc.scalar.copy(dest.bitcast(F32), bank[:].rearrange("p u r -> p r u"))
 
         v_bf = {}
+        pk = {}
 
-        def cast_values(j):
-            v_bf[j] = keep.tile([P, U], BF16, name=f"v_bf{j}", align_bytes=64)
-            for part in range(2):
-                nc.scalar.activation(v_bf[j][:, part * U // 2 : (part + 1) * U // 2], v_raw[j, part][:], ACT.Copy)
+        def cast_values(j, quarters):
+            if j not in v_bf:
+                v_bf[j] = keep.tile([P, U], BF16, name=f"v_bf{j}", align_bytes=64)
+            for quarter in quarters:
+                part, lo_col = divmod(quarter * U // 4, U // 2)
+                nc.scalar.activation(v_bf[j][:, quarter * U // 4 : (quarter + 1) * U // 4], v_raw[j, part][:, lo_col : lo_col + U // 4], ACT.Copy)
 
         def gather_values(j):
-            picked = keep.tile([P, G], BF16, name="pairs1" if j == 3 else f"v_picked{j}", align_bytes=64)
+            picked = keep.tile([P, G], BF16, name=("v_picked0", "v_picked1", "v_picked2", "v_bf2")[j], align_bytes=64)
+            pk[j] = picked
             if j < ON_SCALAR:
                 nc.scalar.activation(picked[:], v_bf[j][:].indirect(entries[:]), ACT.Copy)
             else:
                 nc.vector.tensor_copy(picked[:], v_raw[j][:].indirect(entries[:]))
-            turn(picked, v_in[:, j])
+
+        def turn_values(j):
+            turn(pk[j], v_in[:, j], ("bank7", "bank5", "bank0", "bank3")[j])
 
         def quantize_values(j0, j1):
+            codes = keep.tile([P, (j1 - j0) * P], U32, name="prob1", align_bytes=64)
+            for j in range(j0, j1):
+                v_codes[j] = codes[:, (j - j0) * P : (j - j0 + 1) * P]
             nc.vector.quantize_mx(
-                out=v_codes[:, j0 * P : j1 * P].bitcast(FP8X4),
+                out=codes[:].bitcast(FP8X4),
                 scales=v_scales[:, j0 * P : j1 * P],
                 in_=v_in[:, j0:j1].rearrange("p j e t -> p (j e t)"),
             )
 
-        gw, gs = [], []
+        gs_rows = keep.tile([P, I], U8, name="gs_rows", align_bytes=64)
+        nc.vector.tensor_copy(gs_rows[:], ks[:].indirect(slots[:]))
+        cast_values(0, range(4))
+        gather_values(0)
+        turn_values(0)
+        gs = keep.tile([P, I], U8, name="gs", align_bytes=64)
+        for quad in range(4):
+            nc.sync.dma_start(out=gs[32 * quad : 32 * quad + 4, :].bitcast(I32), in_=gs_rows[112 + 4 * quad : 116 + 4 * quad, :].bitcast(I32))
+        load_values(1, (1,))
+        load_values(2)
+        load_values(3)
+        gw = []
         for half in range(I // HALF):
-            cols = slice(half * HALF // 16, (half + 1) * HALF // 16)
             gw_half = keep.tile([P, HALF], U16, name="q_bf" if half == 1 else "gw0", align_bytes=64)
-            gs_half = keep.tile([P, HALF], U8, name=f"gs{half}", align_bytes=64)
-            nc.vector.tensor_copy(gs_half[:], ks[:].indirect(slots[:, cols]))
-            nc.vector.tensor_copy(gw_half[:], kw[:].indirect(slots[:, cols]))
+            nc.vector.tensor_copy(gw_half[:], kw[:].indirect(slots[:, half * HALF // 16 : (half + 1) * HALF // 16]))
             gw.append(gw_half)
-            gs.append(gs_half)
             if half == 0:
                 nc.vector.quantize_mx(out=q_codes[:].bitcast(FP8X4), scales=q_scales[:], in_=q_bf[:].rearrange("p q j -> p (q j)"))
 
-        cast_values(0)
-        gather_values(0)
-        cast_values(1)
-        gather_values(2)
+        cast_values(1, range(2))
 
-        pairs = [keep.tile([P, 2, G], F32, name=f"pairs{h}", align_bytes=64) for h in range(2)]
+        best = [keep.tile([P, G], F32, name=f"best{h}", align_bytes=64) for h in range(2)]
+
+        order = ((0, 0), (1, 0), (0, 1), (1, 1), (2, 0), (3, 0), (2, 1), (3, 1))
 
         def score(c, h):
             half, lo_col = divmod(c * BANK, HALF)
-            bank = acc_pool.tile([P, BANK], F32, name="acc")
+            bank = psum.tile([P, BANK], F32, name=f"bank{order.index((c, h))}")
             nc.tensor.matmul_mx(
                 out=bank[:],
                 lhsT=q_codes[:, h * P : (h + 1) * P].bitcast(FP8X4),
                 lhsT_scale=q_scales[:, h * P : (h + 1) * P],
                 rhs=gw[half][:, lo_col : lo_col + BANK].bitcast(FP4X4),
-                rhs_scale=gs[half][:, lo_col : lo_col + BANK],
+                rhs_scale=gs[:, c * BANK : (c + 1) * BANK],
                 start=True,
                 stop=True,
             )
-            by_place = bank[:].rearrange("p (g r) -> p r g", r=PACK)
-            low = ring.tile([P, 2, P], F32, name="low", bufs=4)
-            nc.scalar.copy(low[:], by_place[:, 0:2, :])
-            nc.vector.tensor_tensor(pairs[h][:, :, c * P : (c + 1) * P], by_place[:, 2:4, :], low[:], ALU.max)
+            nc.vector.tensor_reduce(best[h][:, c * P : (c + 1) * P], bank[:].rearrange("p (g r) -> p g r", r=PACK), AX.X, ALU.max)
 
-        best, neg_max, prob, total = {}, {}, {}, {}
+        neg_max, prob, total = {}, {}, {}
 
         def softmax(h):
-            best[h] = keep.tile([P, G], F32, name=f"best{h}")[:]
             neg_max[h] = keep.tile([P, 1], F32, name=f"neg_max{h}")
-            prob[h] = keep.tile([P, G], F32, name=f"prob{h}")
+            prob[h] = keep.tile([P, G], F32, name="prob1" if h else "v_bf2", align_bytes=64)
             total[h] = keep.tile([P, 1], F32, name=f"total{h}")
-            nc.vector.tensor_tensor(best[h], pairs[h][:, 0, :], pairs[h][:, 1, :], ALU.max)
-            nc.vector.tensor_reduce(neg_max[h][:], best[h], AX.X, ALU.max, negate=True)
-            nc.scalar.activation(prob[h][:], best[h], ACT.Exp, bias=neg_max[h][:], accum_out=total[h][:])
+            nc.vector.tensor_reduce(neg_max[h][:], best[h][:], AX.X, ALU.max, negate=True)
+            nc.scalar.activation(prob[h][:], best[h][:], ACT.Exp, bias=neg_max[h][:], accum_out=total[h][:])
 
-        w_in = keep.tile([P, 2, P, PACK], BF16, name="w_in", align_bytes=64)
+        w_in = [keep.tile([P, P, PACK], BF16, name=f"w_in{h}", align_bytes=64) for h in range(2)]
         w_codes = keep.tile([P, Q], U32, name="w_codes", align_bytes=64)
         w_scales = keep.tile([P, Q], U8, name="w_scales", align_bytes=64)
 
@@ -176,26 +181,30 @@ def tile_attend_wordmax_pl_kernel(tc, query, keys_words, keys_scales, size, vals
             nc.vector.reciprocal(inv[:], total[h][:])
             w_bf = keep.tile([P, G], BF16, name=f"w_bf{h}", align_bytes=64)
             nc.vector.scalar_tensor_tensor(w_bf[:], prob[h][:], inv[:], size_row[:].rearrange("p m t -> p (m t)"), ALU.mult, ALU.mult)
-            turn(w_bf, w_in[:, h])
+            turn(w_bf, w_in[h][:], ("bank2", "bank4")[h])
 
         def quantize_weights(h):
             cols = slice(h * P, (h + 1) * P)
-            nc.vector.quantize_mx(out=w_codes[:, cols].bitcast(FP8X4), scales=w_scales[:, cols], in_=w_in[:, h].rearrange("p q t -> p (q t)"))
+            nc.vector.quantize_mx(out=w_codes[:, cols].bitcast(FP8X4), scales=w_scales[:, cols], in_=w_in[h][:].rearrange("p q t -> p (q t)"))
 
-        for c, h in ((0, 0), (1, 0), (0, 1), (1, 1), (2, 0), (3, 0)):
+        cast_values(1, range(2, 4))
+        gather_values(1)
+        cast_values(2, range(4))
+        gather_values(2)
+        for c, h in order[:6]:
             score(c, h)
         softmax(0)
-        score(2, 1)
-        score(3, 1)
-        gather_values(1)
-        weigh(0)
+        for c, h in order[6:]:
+            score(c, h)
         softmax(1)
+        turn_values(1)
+        turn_values(2)
+        weigh(0)
         gather_values(3)
-        quantize_values(0, 2)
-        quantize_values(2, 3)
+        turn_values(3)
         quantize_weights(0)
         weigh(1)
-        quantize_values(3, 4)
+        quantize_values(0, 4)
         quantize_weights(1)
 
         o_codes = keep.tile([P, Q], U32, name="o_codes", align_bytes=64)
@@ -204,11 +213,11 @@ def tile_attend_wordmax_pl_kernel(tc, query, keys_words, keys_scales, size, vals
         out_words = out_1[0].rearrange("p q t -> p (q t)").bitcast(I32)
         for h in range(2):
             cols = slice(h * P, (h + 1) * P)
-            bank = acc_pool.tile([P, PACK, P], F32, name="acc")
+            bank = psum.tile([P, PACK, P], F32, name=("bank1", "bank6")[h])
             for j in range(PACK):
                 nc.tensor.matmul_mx(
                     out=bank[:, j, :],
-                    lhsT=v_codes[:, j * P : (j + 1) * P].bitcast(FP8X4),
+                    lhsT=v_codes[j].bitcast(FP8X4),
                     lhsT_scale=v_scales[:, j * P : (j + 1) * P],
                     rhs=w_codes[:, cols].bitcast(FP8X4),
                     rhs_scale=w_scales[:, cols],
@@ -216,15 +225,12 @@ def tile_attend_wordmax_pl_kernel(tc, query, keys_words, keys_scales, size, vals
                     stop=True,
                 )
             o_f32 = keep.tile([P, PACK, P], F32, name=f"o_f32_{h}")
-            o_bf = keep.tile([P, P, PACK], BF16, name=f"o_bf{h}", align_bytes=64)
-            if h == 1:
-                nc.vector.tensor_copy(o_bf[:], bank[:].rearrange("p j q -> p q j"))
+            o_bf = keep.tile([P, P, PACK], BF16, name="o_bf1" if h else "w_in1", align_bytes=64)
+            nc.vector.tensor_copy(o_bf[:], bank[:].rearrange("p j q -> p q j"))
             nc.scalar.copy(o_f32[:], bank[:])
-            nc.sync.dma_start(out=out_rows[:, :, cols], in_=o_f32[:])
-            if h == 0:
-                nc.vector.tensor_copy(o_bf[:], o_f32[:].rearrange("p j q -> p q j"))
+            nc.scalar.dma_start(out=out_rows[:, :, cols], in_=o_f32[:])
             nc.vector.quantize_mx(out=o_codes[:, cols].bitcast(FP8X4), scales=o_scales[:, cols], in_=o_bf[:].rearrange("p q j -> p (q j)"))
             nc.sync.dma_start(out=out_words[:, cols], in_=o_codes[:, cols].bitcast(I32))
         for quad in range(4):
-            queue = nc.scalar if quad % 2 else nc.sync
+            queue = nc.sync
             queue.dma_start(out=out_2[0, 4 * quad : 4 * quad + 4, :].bitcast(I32), in_=o_scales[32 * quad : 32 * quad + 4, :].bitcast(I32))

@@ -20,9 +20,16 @@ AX = mybir.AxisListType
 
 P = 128
 PACK = 4
+TOKENS = I // G
 BANK = 512
-HALF = 1024
+HALF = I // 2
+STRIPE = 16
+BLOCKS = D // 32
+PARKED = P - BLOCKS
 ON_SCALAR = 3
+MX_ALIGN = 64
+
+SCORE_ORDER = tuple((2 * half + chunk, h) for half in range(2) for h in range(2) for chunk in range(2))
 
 
 def tile_attend_wordmax_pl_kernel(tc, query, keys_words, keys_scales, size, vals, offs, offs2, out_0, out_1, out_2):
@@ -31,60 +38,50 @@ def tile_attend_wordmax_pl_kernel(tc, query, keys_words, keys_scales, size, vals
         keep = ctx.enter_context(tc.tile_pool(name="keep", bufs=1))
         psum = ctx.enter_context(tc.psum_pool(name="psum", bufs=1))
 
-        slots = keep.tile([P, I // 16], U16, name="slots")
-        entries = keep.tile([P, G // 16], U16, name="entries")
-        kw = keep.tile([P, T], U16, name="kw", align_bytes=64)
-        ks = keep.tile([P, T], U8, name="ks", align_bytes=64)
-        ks_words = ks[:].bitcast(I32)
-        nc.vector.memset(ks_words[0:112, :], 0)
-        warm = keep.tile([P, 1], F32, name="warm")
-        warm2 = keep.tile([P, 1], F32, name="warm2")
-        nc.vector.memset(warm[:], 0.0)
-        nc.scalar.activation(warm2[:], warm[:], ACT.Exp)
+        slots = keep.tile([P, I // STRIPE], U16, name="slots")
+        entries = keep.tile([P, G // STRIPE], U16, name="entries")
+        key_words = keep.tile([P, T], U16, name="key_words", align_bytes=MX_ALIGN)
+        key_scales = keep.tile([P, T], U8, name="key_scales", align_bytes=MX_ALIGN)
+        key_scales_i32 = key_scales[:].bitcast(I32)
+        nc.vector.memset(key_scales_i32[0:PARKED, :], 0)
 
         size_col = keep.tile([P, PACK], F32, name="size_col")
         nc.sync.dma_start(slots[:], offs)
-        nc.sync.dma_start(out=ks_words[112:128, :], in_=keys_scales[0].bitcast(I32))
+        nc.sync.dma_start(out=key_scales_i32[PARKED:P, :], in_=keys_scales[0].bitcast(I32))
         nc.scalar.dma_start(out=size_col[:], in_=size.rearrange("o (p t) -> (o p) t", t=PACK))
+
         vals_rows = vals.rearrange("(p j) u -> j p u", j=PACK)
         v_raw = {}
 
-        def load_values(j, parts=(0, 1)):
-            if j < ON_SCALAR:
-                for part in parts:
-                    v_part = keep.tile([P, U // 2], F32, name=(("v_part0", "v_part1"), ("v_part2", "ks"), ("v_bf0", "q_raw"))[j][part], align_bytes=64)
-                    nc.sync.dma_start(out=v_part[:], in_=vals_rows[j][:, part * U // 2 : (part + 1) * U // 2])
-                    v_raw[j, part] = v_part
-            else:
-                v_tile = keep.tile([P, U], F32, name="gs_rows", align_bytes=64)
-                nc.sync.dma_start(out=v_tile[:], in_=vals_rows[j])
-                v_raw[j] = v_tile
+        def load_value_half(j, part, buffer):
+            v_raw[j, part] = keep.tile([P, U // 2], F32, name=buffer, align_bytes=MX_ALIGN)
+            nc.sync.dma_start(out=v_raw[j, part][:], in_=vals_rows[j][:, part * U // 2 : (part + 1) * U // 2])
 
-        load_values(0)
+        load_value_half(0, 0, "v_half_a")
+        load_value_half(0, 1, "v_half_b")
         nc.sync.dma_start(entries[:], offs2)
-        nc.sync.dma_start(out=kw[:].bitcast(I32), in_=keys_words[0].bitcast(I32))
-        q_raw = keep.tile([P, PACK, Q], F32, name="q_raw", align_bytes=64)
-        nc.sync.dma_start(out=q_raw[:], in_=query.rearrange("(p j) q -> p j q", j=PACK))
-
-        load_values(1, (0,))
+        nc.sync.dma_start(out=key_words[:].bitcast(I32), in_=keys_words[0].bitcast(I32))
+        q_raw = keep.tile([P, PACK, Q], F32, name="q_raw", align_bytes=MX_ALIGN)
+        nc.sync.dma_start(out=q_raw[:], in_=query.rearrange("(p t) q -> p t q", t=PACK))
+        load_value_half(1, 0, "v_half_c")
 
         ident = keep.tile([P, P], F32, name="ident")
         make_identity(nc, ident[:])
 
-        size_ps = psum.tile([P, PACK, P], F32, name="bank6")
+        size_bank = psum.tile([P, PACK, P], F32, name="bank6")
         for t in range(PACK):
-            nc.tensor.transpose(size_ps[:, t, :], size_col[:, t : t + 1].to_broadcast([P, P]), ident[:])
+            nc.tensor.transpose(size_bank[:, t, :], size_col[:, t : t + 1].to_broadcast([P, P]), ident[:])
         size_row = keep.tile([P, P, PACK], F32, name="size_row")
-        nc.scalar.copy(size_row[:], size_ps[:].rearrange("p t m -> p m t"))
+        nc.scalar.copy(size_row[:], size_bank[:].rearrange("p t m -> p m t"))
 
-        q_bf = keep.tile([P, Q, PACK], BF16, name="q_bf", align_bytes=64)
-        nc.scalar.copy(q_bf[:], q_raw[:].rearrange("p j q -> p q j"))
-        q_codes = keep.tile([P, Q], U32, name="q_codes", align_bytes=64)
-        q_scales = keep.tile([P, Q], U8, name="q_scales", align_bytes=64)
+        q_bf = keep.tile([P, Q, PACK], BF16, name="q_bf", align_bytes=MX_ALIGN)
+        nc.scalar.copy(q_bf[:], q_raw[:].rearrange("p t q -> p q t"))
+        q_codes = keep.tile([P, Q], U32, name="q_codes", align_bytes=MX_ALIGN)
+        q_scales = keep.tile([P, Q], U8, name="q_scales", align_bytes=MX_ALIGN)
 
-        v_in = keep.tile([P, PACK, P, PACK], BF16, name="v_in", align_bytes=64)
-        v_codes = {}
-        v_scales = keep.tile([P, E], U8, name="v_scales", align_bytes=64)
+        v_in = keep.tile([P, PACK, P, PACK], BF16, name="v_in", align_bytes=MX_ALIGN)
+        v_scales = keep.tile([P, E], U8, name="v_scales", align_bytes=MX_ALIGN)
+        v_bf, v_picked, v_codes = {}, {}, {}
 
         def turn(rows_bf, dest, bank_name):
             words = rows_bf[:].bitcast(F32)
@@ -93,131 +90,122 @@ def tile_attend_wordmax_pl_kernel(tc, query, keys_words, keys_scales, size, vals
                 nc.tensor.transpose(bank[:, u, :], words[:, u : G // 2 : 2], ident[:])
             nc.scalar.copy(dest.bitcast(F32), bank[:].rearrange("p u r -> p r u"))
 
-        v_bf = {}
-        pk = {}
+        def gather_values_on_scalar(j):
+            v_bf[j] = keep.tile([P, U], BF16, name=f"v_bf{j}", align_bytes=MX_ALIGN)
+            for quarter in range(4):
+                part, first = divmod(quarter * U // 4, U // 2)
+                nc.scalar.activation(v_bf[j][:, quarter * U // 4 : (quarter + 1) * U // 4], v_raw[j, part][:, first : first + U // 4], ACT.Copy)
+            v_picked[j] = keep.tile([P, G], BF16, name=f"v_picked{j}", align_bytes=MX_ALIGN)
+            nc.scalar.activation(v_picked[j][:], v_bf[j][:].indirect(entries[:]), ACT.Copy)
 
-        def cast_values(j, quarters):
-            if j not in v_bf:
-                v_bf[j] = keep.tile([P, U], BF16, name=f"v_bf{j}", align_bytes=64)
-            for quarter in quarters:
-                part, lo_col = divmod(quarter * U // 4, U // 2)
-                nc.scalar.activation(v_bf[j][:, quarter * U // 4 : (quarter + 1) * U // 4], v_raw[j, part][:, lo_col : lo_col + U // 4], ACT.Copy)
-
-        def gather_values(j):
-            picked = keep.tile([P, G], BF16, name=("v_picked0", "v_picked1", "v_picked2", "v_bf2")[j], align_bytes=64)
-            pk[j] = picked
-            if j < ON_SCALAR:
-                nc.scalar.activation(picked[:], v_bf[j][:].indirect(entries[:]), ACT.Copy)
-            else:
-                nc.vector.tensor_copy(picked[:], v_raw[j][:].indirect(entries[:]))
-
-        def turn_values(j):
-            turn(pk[j], v_in[:, j], ("bank7", "bank5", "bank0", "bank3")[j])
-
-        def quantize_values(j0, j1):
-            codes = keep.tile([P, (j1 - j0) * P], U32, name="prob1", align_bytes=64)
-            for j in range(j0, j1):
-                v_codes[j] = codes[:, (j - j0) * P : (j - j0 + 1) * P]
+        def quantize_values(j, buffer):
+            v_codes[j] = keep.tile([P, P], U32, name=buffer, align_bytes=MX_ALIGN)
             nc.vector.quantize_mx(
-                out=codes[:].bitcast(FP8X4),
-                scales=v_scales[:, j0 * P : j1 * P],
-                in_=v_in[:, j0:j1].rearrange("p j e t -> p (j e t)"),
+                out=v_codes[j][:].bitcast(FP8X4),
+                scales=v_scales[:, j * P : (j + 1) * P],
+                in_=v_in[:, j].rearrange("p m t -> p (m t)"),
             )
 
-        gs_rows = keep.tile([P, I], U8, name="gs_rows", align_bytes=64)
-        nc.vector.tensor_copy(gs_rows[:], ks[:].indirect(slots[:]))
-        cast_values(0, range(4))
-        gather_values(0)
-        turn_values(0)
-        gs = keep.tile([P, I], U8, name="gs", align_bytes=64)
+        parked_scales = keep.tile([P, I], U8, name="parked_scales", align_bytes=MX_ALIGN)
+        nc.vector.tensor_copy(parked_scales[:], key_scales[:].indirect(slots[:]))
+        gather_values_on_scalar(0)
+        slot_scales = keep.tile([P, I], U8, name="slot_scales", align_bytes=MX_ALIGN)
         for quad in range(4):
-            nc.sync.dma_start(out=gs[32 * quad : 32 * quad + 4, :].bitcast(I32), in_=gs_rows[112 + 4 * quad : 116 + 4 * quad, :].bitcast(I32))
-        load_values(1, (1,))
-        load_values(2)
-        load_values(3)
-        gw = []
-        for half in range(I // HALF):
-            gw_half = keep.tile([P, HALF], U16, name="q_bf" if half == 1 else "gw0", align_bytes=64)
-            nc.vector.tensor_copy(gw_half[:], kw[:].indirect(slots[:, half * HALF // 16 : (half + 1) * HALF // 16]))
-            gw.append(gw_half)
+            nc.sync.dma_start(
+                out=slot_scales[32 * quad : 32 * quad + 4, :].bitcast(I32),
+                in_=parked_scales[PARKED + 4 * quad : PARKED + 4 * quad + 4, :].bitcast(I32),
+            )
+
+        load_value_half(1, 1, "key_scales")
+        load_value_half(2, 0, "v_bf0")
+        load_value_half(2, 1, "parked_scales")
+        v_last = keep.tile([P, U], F32, name="q_raw", align_bytes=MX_ALIGN)
+        nc.sync.dma_start(out=v_last[:], in_=vals_rows[ON_SCALAR])
+
+        slot_words = []
+        for half, buffer in enumerate(("slot_words0", "q_bf")):
+            words_half = keep.tile([P, HALF], U16, name=buffer, align_bytes=MX_ALIGN)
+            nc.vector.tensor_copy(words_half[:], key_words[:].indirect(slots[:, half * HALF // STRIPE : (half + 1) * HALF // STRIPE]))
+            slot_words.append(words_half)
             if half == 0:
-                nc.vector.quantize_mx(out=q_codes[:].bitcast(FP8X4), scales=q_scales[:], in_=q_bf[:].rearrange("p q j -> p (q j)"))
+                nc.vector.quantize_mx(out=q_codes[:].bitcast(FP8X4), scales=q_scales[:], in_=q_bf[:].rearrange("p q t -> p (q t)"))
 
-        cast_values(1, range(2))
+        best = [keep.tile([P, G], F32, name=f"best{h}", align_bytes=MX_ALIGN) for h in range(2)]
 
-        best = [keep.tile([P, G], F32, name=f"best{h}", align_bytes=64) for h in range(2)]
-
-        order = ((0, 0), (1, 0), (0, 1), (1, 1), (2, 0), (3, 0), (2, 1), (3, 1))
-
-        def score(c, h):
-            half, lo_col = divmod(c * BANK, HALF)
-            bank = psum.tile([P, BANK], F32, name=f"bank{order.index((c, h))}")
+        def score(n):
+            chunk, h = SCORE_ORDER[n]
+            half, first = divmod(chunk * BANK, HALF)
+            bank = psum.tile([P, BANK], F32, name=f"bank{n}")
             nc.tensor.matmul_mx(
                 out=bank[:],
                 lhsT=q_codes[:, h * P : (h + 1) * P].bitcast(FP8X4),
                 lhsT_scale=q_scales[:, h * P : (h + 1) * P],
-                rhs=gw[half][:, lo_col : lo_col + BANK].bitcast(FP4X4),
-                rhs_scale=gs[:, c * BANK : (c + 1) * BANK],
+                rhs=slot_words[half][:, first : first + BANK].bitcast(FP4X4),
+                rhs_scale=slot_scales[:, chunk * BANK : (chunk + 1) * BANK],
                 start=True,
                 stop=True,
             )
-            nc.vector.tensor_reduce(best[h][:, c * P : (c + 1) * P], bank[:].rearrange("p (g r) -> p g r", r=PACK), AX.X, ALU.max)
+            words_here = slice(chunk * BANK // TOKENS, (chunk + 1) * BANK // TOKENS)
+            nc.vector.tensor_reduce(best[h][:, words_here], bank[:].rearrange("p (g r) -> p g r", r=TOKENS), AX.X, ALU.max)
 
-        neg_max, prob, total = {}, {}, {}
+        prob, total = {}, {}
 
-        def softmax(h):
-            neg_max[h] = keep.tile([P, 1], F32, name=f"neg_max{h}")
-            prob[h] = keep.tile([P, G], F32, name="prob1" if h else "v_bf2", align_bytes=64)
+        def softmax(h, buffer):
+            neg_max = keep.tile([P, 1], F32, name=f"neg_max{h}")
+            prob[h] = keep.tile([P, G], F32, name=buffer, align_bytes=MX_ALIGN)
             total[h] = keep.tile([P, 1], F32, name=f"total{h}")
-            nc.vector.tensor_reduce(neg_max[h][:], best[h][:], AX.X, ALU.max, negate=True)
-            nc.scalar.activation(prob[h][:], best[h][:], ACT.Exp, bias=neg_max[h][:], accum_out=total[h][:])
+            nc.vector.tensor_reduce(neg_max[:], best[h][:], AX.X, ALU.max, negate=True)
+            nc.scalar.activation(prob[h][:], best[h][:], ACT.Exp, bias=neg_max[:], accum_out=total[h][:])
 
-        w_in = [keep.tile([P, P, PACK], BF16, name=f"w_in{h}", align_bytes=64) for h in range(2)]
-        w_codes = keep.tile([P, Q], U32, name="w_codes", align_bytes=64)
-        w_scales = keep.tile([P, Q], U8, name="w_scales", align_bytes=64)
+        w_in = [keep.tile([P, P, PACK], BF16, name=f"w_in{h}", align_bytes=MX_ALIGN) for h in range(2)]
+        w_codes = keep.tile([P, Q], U32, name="w_codes", align_bytes=MX_ALIGN)
+        w_scales = keep.tile([P, Q], U8, name="w_scales", align_bytes=MX_ALIGN)
 
-        def weigh(h):
-            inv = keep.tile([P, 1], F32, name=f"inv{h}")
-            nc.vector.reciprocal(inv[:], total[h][:])
-            w_bf = keep.tile([P, G], BF16, name=f"w_bf{h}", align_bytes=64)
-            nc.vector.scalar_tensor_tensor(w_bf[:], prob[h][:], inv[:], size_row[:].rearrange("p m t -> p (m t)"), ALU.mult, ALU.mult)
-            turn(w_bf, w_in[h][:], ("bank2", "bank4")[h])
+        def weigh(h, bank_name):
+            inv_total = keep.tile([P, 1], F32, name=f"inv_total{h}")
+            nc.vector.reciprocal(inv_total[:], total[h][:])
+            w_bf = keep.tile([P, G], BF16, name=f"w_bf{h}", align_bytes=MX_ALIGN)
+            nc.vector.scalar_tensor_tensor(w_bf[:], prob[h][:], inv_total[:], size_row[:].rearrange("p m t -> p (m t)"), ALU.mult, ALU.mult)
+            turn(w_bf, w_in[h][:], bank_name)
 
         def quantize_weights(h):
             cols = slice(h * P, (h + 1) * P)
             nc.vector.quantize_mx(out=w_codes[:, cols].bitcast(FP8X4), scales=w_scales[:, cols], in_=w_in[h][:].rearrange("p q t -> p (q t)"))
 
-        cast_values(1, range(2, 4))
-        gather_values(1)
-        cast_values(2, range(4))
-        gather_values(2)
-        for c, h in order[:6]:
-            score(c, h)
-        softmax(0)
-        for c, h in order[6:]:
-            score(c, h)
-        softmax(1)
-        turn_values(1)
-        turn_values(2)
-        weigh(0)
-        gather_values(3)
-        turn_values(3)
+        for j in range(1, ON_SCALAR):
+            gather_values_on_scalar(j)
+        last_of_tile_0 = SCORE_ORDER.index((I // BANK - 1, 0))
+        for n in range(len(SCORE_ORDER)):
+            score(n)
+            if n == last_of_tile_0:
+                softmax(0, "v_bf2")
+        softmax(1, "prob1")
+
+        for j, bank_name in enumerate(("bank0", "bank5", "bank7")):
+            turn(v_picked[j], v_in[:, j], bank_name)
+        weigh(0, "bank2")
+
+        v_picked[ON_SCALAR] = keep.tile([P, G], BF16, name="v_bf2", align_bytes=MX_ALIGN)
+        nc.vector.tensor_copy(v_picked[ON_SCALAR][:], v_last[:].indirect(entries[:]))
+        turn(v_picked[ON_SCALAR], v_in[:, ON_SCALAR], "bank3")
         quantize_weights(0)
-        weigh(1)
-        quantize_values(0, 4)
+        weigh(1, "bank4")
+        for j in range(ON_SCALAR):
+            quantize_values(j, f"v_codes{j}")
+        quantize_values(ON_SCALAR, "prob1")
         quantize_weights(1)
 
-        o_codes = keep.tile([P, Q], U32, name="o_codes", align_bytes=64)
-        o_scales = keep.tile([P, Q], U8, name="o_scales", align_bytes=64)
+        o_codes = keep.tile([P, Q], U32, name="o_codes", align_bytes=MX_ALIGN)
+        o_scales = keep.tile([P, Q], U8, name="o_scales", align_bytes=MX_ALIGN)
         out_rows = out_0.rearrange("(p j) q -> p j q", j=PACK)
         out_words = out_1[0].rearrange("p q t -> p (q t)").bitcast(I32)
-        for h in range(2):
+        for h, (bank_name, buffer) in enumerate((("bank1", "w_in1"), ("bank6", "o_bf1"))):
             cols = slice(h * P, (h + 1) * P)
-            bank = psum.tile([P, PACK, P], F32, name=("bank1", "bank6")[h])
+            bank = psum.tile([P, PACK, P], F32, name=bank_name)
             for j in range(PACK):
                 nc.tensor.matmul_mx(
                     out=bank[:, j, :],
-                    lhsT=v_codes[j].bitcast(FP8X4),
+                    lhsT=v_codes[j][:].bitcast(FP8X4),
                     lhsT_scale=v_scales[:, j * P : (j + 1) * P],
                     rhs=w_codes[:, cols].bitcast(FP8X4),
                     rhs_scale=w_scales[:, cols],
@@ -225,12 +213,15 @@ def tile_attend_wordmax_pl_kernel(tc, query, keys_words, keys_scales, size, vals
                     stop=True,
                 )
             o_f32 = keep.tile([P, PACK, P], F32, name=f"o_f32_{h}")
-            o_bf = keep.tile([P, P, PACK], BF16, name="o_bf1" if h else "w_in1", align_bytes=64)
+            o_bf = keep.tile([P, P, PACK], BF16, name=buffer, align_bytes=MX_ALIGN)
             nc.vector.tensor_copy(o_bf[:], bank[:].rearrange("p j q -> p q j"))
             nc.scalar.copy(o_f32[:], bank[:])
             nc.scalar.dma_start(out=out_rows[:, :, cols], in_=o_f32[:])
             nc.vector.quantize_mx(out=o_codes[:, cols].bitcast(FP8X4), scales=o_scales[:, cols], in_=o_bf[:].rearrange("p q j -> p (q j)"))
             nc.sync.dma_start(out=out_words[:, cols], in_=o_codes[:, cols].bitcast(I32))
+
         for quad in range(4):
-            queue = nc.sync
-            queue.dma_start(out=out_2[0, 4 * quad : 4 * quad + 4, :].bitcast(I32), in_=o_scales[32 * quad : 32 * quad + 4, :].bitcast(I32))
+            nc.sync.dma_start(
+                out=out_2[0, 4 * quad : 4 * quad + 4, :].bitcast(I32),
+                in_=o_scales[32 * quad : 32 * quad + 4, :].bitcast(I32),
+            )

from contextlib import ExitStack

import concourse.mybir as mybir
from concourse.masks import make_identity

D, T, I, G, U, Q, E = 512, 4096, 2048, 512, 2048, 256, 512
FLOPS = 2 * Q * I * D + 2 * E * Q * G

F32 = mybir.dt.float32
BF16 = mybir.dt.bfloat16
I32 = mybir.dt.int32
U32 = mybir.dt.uint32
U16 = mybir.dt.uint16
U8 = mybir.dt.uint8
FP8X4 = mybir.dt.float8_e4m3fn_x4
FP4X4 = mybir.dt.float4_e2m1fn_x4
ALU = mybir.AluOpType
ACT = mybir.ActivationFunctionType
AX = mybir.AxisListType

P = 128
PACK = 4
TOKENS = I // G
BANK = 512
HALF = I // 2
STRIPE = 16
BLOCKS = D // 32
PARKED = P - BLOCKS
ON_SCALAR = 3
MX_ALIGN = 64

SCORE_ORDER = tuple((2 * half + chunk, h) for half in range(2) for h in range(2) for chunk in range(2))


def tile_attend_wordmax_pl_kernel(tc, query, keys_words, keys_scales, size, vals, offs, offs2, out_0, out_1, out_2):
    nc = tc.nc
    with ExitStack() as ctx:
        keep = ctx.enter_context(tc.tile_pool(name="keep", bufs=1))
        psum = ctx.enter_context(tc.psum_pool(name="psum", bufs=1))

        slots = keep.tile([P, I // STRIPE], U16, name="slots")
        entries = keep.tile([P, G // STRIPE], U16, name="entries")
        key_words = keep.tile([P, T], U16, name="key_words", align_bytes=MX_ALIGN)
        key_scales = keep.tile([P, T], U8, name="key_scales", align_bytes=MX_ALIGN)
        key_scales_i32 = key_scales[:].bitcast(I32)
        nc.vector.memset(key_scales_i32[0:PARKED, :], 0)

        size_col = keep.tile([P, PACK], F32, name="size_col")
        nc.sync.dma_start(slots[:], offs)
        nc.sync.dma_start(out=key_scales_i32[PARKED:P, :], in_=keys_scales[0].bitcast(I32))
        nc.scalar.dma_start(out=size_col[:], in_=size.rearrange("o (p t) -> (o p) t", t=PACK))

        vals_rows = vals.rearrange("(p j) u -> j p u", j=PACK)
        v_raw = {}

        def load_value_half(j, part, buffer):
            v_raw[j, part] = keep.tile([P, U // 2], F32, name=buffer, align_bytes=MX_ALIGN)
            nc.sync.dma_start(out=v_raw[j, part][:], in_=vals_rows[j][:, part * U // 2 : (part + 1) * U // 2])

        load_value_half(0, 0, "v_half_a")
        load_value_half(0, 1, "v_half_b")
        nc.sync.dma_start(entries[:], offs2)
        nc.sync.dma_start(out=key_words[:].bitcast(I32), in_=keys_words[0].bitcast(I32))
        q_raw = keep.tile([P, PACK, Q], F32, name="q_raw", align_bytes=MX_ALIGN)
        nc.sync.dma_start(out=q_raw[:], in_=query.rearrange("(p t) q -> p t q", t=PACK))
        load_value_half(1, 0, "v_half_c")

        ident = keep.tile([P, P], F32, name="ident")
        make_identity(nc, ident[:])

        size_bank = psum.tile([P, PACK, P], F32, name="bank6")
        for t in range(PACK):
            nc.tensor.transpose(size_bank[:, t, :], size_col[:, t : t + 1].to_broadcast([P, P]), ident[:])
        size_row = keep.tile([P, P, PACK], F32, name="size_row")
        nc.scalar.copy(size_row[:], size_bank[:].rearrange("p t m -> p m t"))

        q_bf = keep.tile([P, Q, PACK], BF16, name="q_bf", align_bytes=MX_ALIGN)
        nc.scalar.copy(q_bf[:], q_raw[:].rearrange("p t q -> p q t"))
        q_codes = keep.tile([P, Q], U32, name="q_codes", align_bytes=MX_ALIGN)
        q_scales = keep.tile([P, Q], U8, name="q_scales", align_bytes=MX_ALIGN)

        v_in = keep.tile([P, PACK, P, PACK], BF16, name="v_in", align_bytes=MX_ALIGN)
        v_scales = keep.tile([P, E], U8, name="v_scales", align_bytes=MX_ALIGN)
        v_bf, v_picked, v_codes = {}, {}, {}

        def turn(rows_bf, dest, bank_name):
            words = rows_bf[:].bitcast(F32)
            bank = psum.tile([P, 2, P], F32, name=bank_name)
            for u in range(2):
                nc.tensor.transpose(bank[:, u, :], words[:, u : G // 2 : 2], ident[:])
            nc.scalar.copy(dest.bitcast(F32), bank[:].rearrange("p u r -> p r u"))

        def gather_values_on_scalar(j):
            v_bf[j] = keep.tile([P, U], BF16, name=f"v_bf{j}", align_bytes=MX_ALIGN)
            for quarter in range(4):
                part, first = divmod(quarter * U // 4, U // 2)
                nc.scalar.activation(v_bf[j][:, quarter * U // 4 : (quarter + 1) * U // 4], v_raw[j, part][:, first : first + U // 4], ACT.Copy)
            v_picked[j] = keep.tile([P, G], BF16, name=f"v_picked{j}", align_bytes=MX_ALIGN)
            nc.scalar.activation(v_picked[j][:], v_bf[j][:].indirect(entries[:]), ACT.Copy)

        def quantize_values(j, buffer):
            v_codes[j] = keep.tile([P, P], U32, name=buffer, align_bytes=MX_ALIGN)
            nc.vector.quantize_mx(
                out=v_codes[j][:].bitcast(FP8X4),
                scales=v_scales[:, j * P : (j + 1) * P],
                in_=v_in[:, j].rearrange("p m t -> p (m t)"),
            )

        parked_scales = keep.tile([P, I], U8, name="parked_scales", align_bytes=MX_ALIGN)
        nc.vector.tensor_copy(parked_scales[:], key_scales[:].indirect(slots[:]))
        gather_values_on_scalar(0)
        slot_scales = keep.tile([P, I], U8, name="slot_scales", align_bytes=MX_ALIGN)
        for quad in range(4):
            nc.sync.dma_start(
                out=slot_scales[32 * quad : 32 * quad + 4, :].bitcast(I32),
                in_=parked_scales[PARKED + 4 * quad : PARKED + 4 * quad + 4, :].bitcast(I32),
            )

        load_value_half(1, 1, "key_scales")
        load_value_half(2, 0, "v_bf0")
        load_value_half(2, 1, "parked_scales")
        v_last = keep.tile([P, U], F32, name="q_raw", align_bytes=MX_ALIGN)
        nc.sync.dma_start(out=v_last[:], in_=vals_rows[ON_SCALAR])

        slot_words = []
        for half, buffer in enumerate(("slot_words0", "q_bf")):
            words_half = keep.tile([P, HALF], U16, name=buffer, align_bytes=MX_ALIGN)
            nc.vector.tensor_copy(words_half[:], key_words[:].indirect(slots[:, half * HALF // STRIPE : (half + 1) * HALF // STRIPE]))
            slot_words.append(words_half)
            if half == 0:
                nc.vector.quantize_mx(out=q_codes[:].bitcast(FP8X4), scales=q_scales[:], in_=q_bf[:].rearrange("p q t -> p (q t)"))

        best = [keep.tile([P, G], F32, name=f"best{h}", align_bytes=MX_ALIGN) for h in range(2)]

        def score(n):
            chunk, h = SCORE_ORDER[n]
            half, first = divmod(chunk * BANK, HALF)
            bank = psum.tile([P, BANK], F32, name=f"bank{n}")
            nc.tensor.matmul_mx(
                out=bank[:],
                lhsT=q_codes[:, h * P : (h + 1) * P].bitcast(FP8X4),
                lhsT_scale=q_scales[:, h * P : (h + 1) * P],
                rhs=slot_words[half][:, first : first + BANK].bitcast(FP4X4),
                rhs_scale=slot_scales[:, chunk * BANK : (chunk + 1) * BANK],
                start=True,
                stop=True,
            )
            words_here = slice(chunk * BANK // TOKENS, (chunk + 1) * BANK // TOKENS)
            nc.vector.tensor_reduce(best[h][:, words_here], bank[:].rearrange("p (g r) -> p g r", r=TOKENS), AX.X, ALU.max)

        prob, total = {}, {}

        def softmax(h, buffer):
            neg_max = keep.tile([P, 1], F32, name=f"neg_max{h}")
            prob[h] = keep.tile([P, G], F32, name=buffer, align_bytes=MX_ALIGN)
            total[h] = keep.tile([P, 1], F32, name=f"total{h}")
            nc.vector.tensor_reduce(neg_max[:], best[h][:], AX.X, ALU.max, negate=True)
            nc.scalar.activation(prob[h][:], best[h][:], ACT.Exp, bias=neg_max[:], accum_out=total[h][:])

        w_in = [keep.tile([P, P, PACK], BF16, name=f"w_in{h}", align_bytes=MX_ALIGN) for h in range(2)]
        w_codes = keep.tile([P, Q], U32, name="w_codes", align_bytes=MX_ALIGN)
        w_scales = keep.tile([P, Q], U8, name="w_scales", align_bytes=MX_ALIGN)

        def weigh(h, bank_name):
            inv_total = keep.tile([P, 1], F32, name=f"inv_total{h}")
            nc.vector.reciprocal(inv_total[:], total[h][:])
            w_bf = keep.tile([P, G], BF16, name=f"w_bf{h}", align_bytes=MX_ALIGN)
            nc.vector.scalar_tensor_tensor(w_bf[:], prob[h][:], inv_total[:], size_row[:].rearrange("p m t -> p (m t)"), ALU.mult, ALU.mult)
            turn(w_bf, w_in[h][:], bank_name)

        def quantize_weights(h):
            cols = slice(h * P, (h + 1) * P)
            nc.vector.quantize_mx(out=w_codes[:, cols].bitcast(FP8X4), scales=w_scales[:, cols], in_=w_in[h][:].rearrange("p q t -> p (q t)"))

        for j in range(1, ON_SCALAR):
            gather_values_on_scalar(j)
        last_of_tile_0 = SCORE_ORDER.index((I // BANK - 1, 0))
        for n in range(len(SCORE_ORDER)):
            score(n)
            if n == last_of_tile_0:
                softmax(0, "v_bf2")
        softmax(1, "prob1")

        for j, bank_name in enumerate(("bank0", "bank5", "bank7")):
            turn(v_picked[j], v_in[:, j], bank_name)
        weigh(0, "bank2")

        v_picked[ON_SCALAR] = keep.tile([P, G], BF16, name="v_bf2", align_bytes=MX_ALIGN)
        nc.vector.tensor_copy(v_picked[ON_SCALAR][:], v_last[:].indirect(entries[:]))
        turn(v_picked[ON_SCALAR], v_in[:, ON_SCALAR], "bank3")
        quantize_weights(0)
        weigh(1, "bank4")
        for j in range(ON_SCALAR):
            quantize_values(j, f"v_codes{j}")
        quantize_values(ON_SCALAR, "prob1")
        quantize_weights(1)

        o_codes = keep.tile([P, Q], U32, name="o_codes", align_bytes=MX_ALIGN)
        o_scales = keep.tile([P, Q], U8, name="o_scales", align_bytes=MX_ALIGN)
        out_rows = out_0.rearrange("(p j) q -> p j q", j=PACK)
        out_words = out_1[0].rearrange("p q t -> p (q t)").bitcast(I32)
        for h, (bank_name, buffer) in enumerate((("bank1", "w_in1"), ("bank6", "o_bf1"))):
            cols = slice(h * P, (h + 1) * P)
            bank = psum.tile([P, PACK, P], F32, name=bank_name)
            for j in range(PACK):
                nc.tensor.matmul_mx(
                    out=bank[:, j, :],
                    lhsT=v_codes[j][:].bitcast(FP8X4),
                    lhsT_scale=v_scales[:, j * P : (j + 1) * P],
                    rhs=w_codes[:, cols].bitcast(FP8X4),
                    rhs_scale=w_scales[:, cols],
                    start=True,
                    stop=True,
                )
            o_f32 = keep.tile([P, PACK, P], F32, name=f"o_f32_{h}")
            o_bf = keep.tile([P, P, PACK], BF16, name=buffer, align_bytes=MX_ALIGN)
            nc.vector.tensor_copy(o_bf[:], bank[:].rearrange("p j q -> p q j"))
            nc.scalar.copy(o_f32[:], bank[:])
            nc.scalar.dma_start(out=out_rows[:, :, cols], in_=o_f32[:])
            nc.vector.quantize_mx(out=o_codes[:, cols].bitcast(FP8X4), scales=o_scales[:, cols], in_=o_bf[:].rearrange("p q j -> p (q j)"))
            nc.sync.dma_start(out=out_words[:, cols], in_=o_codes[:, cols].bitcast(I32))

        for quad in range(4):
            nc.sync.dma_start(
                out=out_2[0, 4 * quad : 4 * quad + 4, :].bitcast(I32),
                in_=o_scales[32 * quad : 32 * quad + 4, :].bitcast(I32),
            )
